import numpy as np, ml_dtypes
CORES = [17,57,65,89,97,121]
N = 6
import mx_ref
NC, G = 256, 4
C = np.float32(0.023)
BF = ml_dtypes.bfloat16
def cut(t, i, w=512):
    return t[:, w * i:w * i + w]
def tile(rs):
    return np.stack(rs, axis=2).reshape(128, -1).astype(BF)
def layer(w, X):
    out = []
    for i in range(G):
        for t in range(len(X)):
            p = mx_ref.matmul(mx_ref.quantize(cut(w, len(X) * i + t)), X[t])
            z = p if t == 0 else z + p
        out.append(z)
    return out
def act(Z):
    return [np.maximum(z, 0) * C for z in Z]
def setup_inputs(rng):
    def f(*shape):
        return mx_ref.flush((rng.standard_normal(shape, dtype=np.float32) * np.exp2(rng.integers(-2, 3, shape[:-1] + (1,)))).astype(BF))
    return {"x": f(N, 128, 4 * NC), "w1": f(N, 128, G * 512), "w2": f(N, 128, 512)}
def setup_inputs_blocks(rng):
    d = setup_inputs(rng)
    for k in ("x", "w1", "w2"): d[k] = mx_ref.spread(d[k], rng, 4)
    return d
def setup_inputs_wide(rng):
    d = setup_inputs(rng)
    for k in ("x", "w1", "w2"): d[k] = mx_ref.flush((d[k].astype(np.float32) * np.exp2(rng.integers(-8, 9, (N, 1, 1))).astype(np.float32)).astype(BF))
    return d
def setup_inputs_zeros(rng):
    d = setup_inputs(rng); v = d["x"].reshape(N, 128, -1, 4).copy()
    v[np.broadcast_to((rng.random((N, 1, v.shape[2], 1)) < 0.33), v.shape)] = 0
    d["x"] = v.reshape(d["x"].shape)
    return d
def reference(x, w1, w2):
    H = [mx_ref.quantize(tile(act(layer(w1[j], [mx_ref.quantize(x[j])])))) for j in range(N)]
    y = np.full((N, 128, N * NC), np.nan, np.float32)
    for r in range(N):
        qw = mx_ref.quantize(w2[r])
        for j in range(r + 1):
            y[r][:, NC * j:NC * j + NC] = mx_ref.matmul(qw, H[j])
    return {"y": y}

@@ -1,0 +1,200 @@
+from concourse.bass import DstId, RemoteDMATransfer
+from concourse.mybir import dt, AluOpType, ActivationFunctionType
+
+N = 6
+NC = 256
+G = 4
+WC = 128
+C = 0.023
+BANK = 512
+NBANKS = 8
+
+OWN_DIE = {(0, 5): False, (0, 3): True, (0, 1): True,
+           (1, 4): False, (1, 2): True,
+           (2, 5): True, (2, 3): False,
+           (3, 4): False,
+           (4, 5): False}
+ENGINES = 8
+
+RUNS = [(0, 0, NC), (1, 0, NC), (2, 0, NC), (3, 0, NC // 2), (3, NC // 2, NC)]
+
+SCRATCH = {
+    "xb": ("sbuf", [128, 4 * NC], "bfloat16"),
+    "w1b": ("sbuf", [128, G * 4 * WC], "bfloat16"),
+    "w2b": ("sbuf", [128, 4 * WC], "bfloat16"),
+    "hb": ("sbuf", [128, 4 * NC], "bfloat16"),
+    "xq": ("sbuf", [128, NC], "float8_e4m3fn_x4"),
+    "xs": ("sbuf", [128, NC], "uint8"),
+    "w1q": ("sbuf", [128, G * WC], "float8_e4m3fn_x4"),
+    "w1s": ("sbuf", [128, G * WC], "uint8"),
+    "w2q": ("sbuf", [128, WC], "float8_e4m3fn_x4"),
+    "w2s": ("sbuf", [128, WC], "uint8"),
+    "gq": ("sbuf", [128, N * NC], "float8_e4m3fn_x4"),
+    "gs": ("sbuf", [128, N * NC], "uint8"),
+    "ysb": ("sbuf", [128, N * NC], "float32"),
+    "ps": ("psum", [128, NBANKS * BANK], "float32"),
+}
+SEMAPHORES = (["ld_x", "ld_wa", "ld_wb", "ld_w2", "q_x", "q_v", "q_h", "sent"]
+              + ["q_w%d" % i for i in range(G)]
+              + ["z%d" % k for k in range(len(RUNS))] + ["a%d" % k for k in range(len(RUNS))]
+              + ["as%d" % j for j in range(N)] + ["aq%d" % j for j in range(N)]
+              + ["m%d" % j for j in range(N)] + ["c%d" % j for j in range(N)] + ["st%d" % j for j in range(N)])
+
+
+def _count(mask):
+    return bin(mask).count("1")
+
+
+def _take(mask, k):
+    out = 0
+    for e in range(mask.bit_length()):
+        if (mask >> e) & 1 and _count(out) < k:
+            out |= 1 << e
+    return out
+
+
+def _plan(T, topo):
+    cores = list(T.cores)
+    every = range(topo.CHIPS * topo.CORES_PER_CHIP)
+    sends, relays, arrive = {}, {}, dict((r, {}) for r in range(N))
+    for j, src in enumerate(cores):
+        groups, queued = [], [0, 0]
+        direct = [r for r in range(N - 1, j, -1) if topo.may_write(src, cores[r])]
+        for n, r in enumerate(r for r in range(N - 1, j, -1) if r not in direct):
+            dst = cores[r]
+            relay = [c for c in every
+                     if topo.chip(c) == topo.chip(src) and T.rank_of(c) is None and c not in relays
+                     and topo.may_write(c, dst) and (topo.die(c) == topo.die(src)) == OWN_DIE[(j, r)]][0]
+            s = n % 2
+            leave = topo.mask(src, dst)
+            mask = _take(topo.mask(src, relay) & (leave if s else ~leave), ENGINES)
+            out = _take(topo.mask(relay, dst), ENGINES)
+            relays[relay] = (j, dst, _count(mask), out)
+            groups.append((mask, [relay]))
+            queued[s] += 1
+            arrive[r][j] = (_count(out), queued[s] + 4.0 - 0.01 * j)
+        if direct:
+            mask = _take(topo.mask(src, cores[direct[0]]), ENGINES)
+            groups.append((mask, [cores[r] for r in direct]))
+            for r in direct:
+                queued[1] += 1
+                arrive[r][j] = (_count(mask), queued[1] + 1.5 - 0.01 * j)
+        sends[j] = groups
+    return sends, relays, arrive
+
+
+def _slot(j):
+    return slice(NC * j, NC * j + NC)
+
+
+def _write(g, T, topo, j, what, mask, dests, local_sem):
+    if what == "s":
+        view, sem = T.gs[:, _slot(j)], T.sem["as%d" % j]
+    else:
+        view, sem = T.gq[:, _slot(j)].bitcast(dt.uint8), T.sem["aq%d" % j]
+    if len(dests) == 1:
+        rid, pid, _ = topo.addr(dests[0])
+        g.remote_dma(out_ap=view, in_ap=view, remote_sem=sem, local_sem=local_sem, pid=pid, routing_id=rid,
+                     dma_engine_mask=mask)
+    else:
+        ids = [DstId(rid=topo.addr(d)[0], pnc=topo.addr(d)[1]) for d in dests]
+        g.remote_dma_fused([RemoteDMATransfer(dst_ids=ids, dma_engine_mask=mask, remote_sem=sem, srcs=[view],
+                                              dsts=[view for _ in dests])], local_sem=local_sem)
+    return _count(mask)
+
+
+def _relay(g, T, topo, job):
+    j, dst, n_in, out = job
+    left = 0
+    for what in ("s", "q"):
+        g.wait_ge(T.sem["a%s%d" % (what, j)], n_in)
+        left += _write(g, T, topo, j, what, out, [dst], T.sem.sent)
+    g.wait_ge(T.sem.sent, left)
+
+
+def _rank(g, T, topo, r, groups, arrive):
+    S = T.sem
+    v, t, sc, sy = g.vector, g.tensor, g.scalar, g.sync
+    half = G * 4 * WC // 2
+
+    sy.dma_start(T.xb[:], T.x[:]).then_inc(S.ld_x, 16)
+    sc.dma_start(T.w1b[:, 0:half], T.w1[:, 0:half]).then_inc(S.ld_wa, 16)
+    sy.dma_start(T.w1b[:, half:2 * half], T.w1[:, half:2 * half]).then_inc(S.ld_wb, 16)
+    sc.dma_start(T.w2b[:], T.w2[:]).then_inc(S.ld_w2, 16)
+
+    v.wait_ge(S.ld_x, 16)
+    v.quantize_mx(T.xq[:], T.xs[:], T.xb[:]).then_inc(S.q_x, 1)
+    for i in range(G):
+        if i == 0:
+            v.wait_ge(S.ld_wa, 16)
+        if i == G // 2:
+            v.wait_ge(S.ld_wb, 16)
+        v.quantize_mx(T.w1q[:, WC * i:WC * i + WC], T.w1s[:, WC * i:WC * i + WC],
+                      T.w1b[:, 4 * WC * i:4 * WC * i + 4 * WC]).then_inc(S["q_w%d" % i], 1)
+
+    t.wait_ge(S.q_x, 1)
+    for k, (b, c0, c1) in enumerate(RUNS):
+        if c0 == 0:
+            t.wait_ge(S["q_w%d" % b], 1)
+        z = T.ps[:, BANK * k:BANK * k + (c1 - c0)]
+        t.matmul_mx(z, T.w1q[:, WC * b:WC * b + WC], T.w1s[:, WC * b:WC * b + WC],
+                    T.xq[:, c0:c1], T.xs[:, c0:c1], True, True).then_inc(S["z%d" % k], 1)
+        h = T.hb[:, 4 * c0 + b:4 * c1:4]
+        if k < len(RUNS) - 1:
+            sc.wait_ge(S["z%d" % k], 1)
+            sc.activation(h, z, ActivationFunctionType.Relu, scale=C).then_inc(S["a%d" % k], 1)
+        else:
+            v.wait_ge(S["z%d" % k], 1)
+            v.tensor_scalar(h, z, 0.0, C, AluOpType.max, AluOpType.mult).then_inc(S["a%d" % k], 1)
+    for k in range(len(RUNS)):
+        v.wait_ge(S["a%d" % k], 1)
+    v.quantize_mx(T.gq[:, _slot(r)], T.gs[:, _slot(r)], T.hb[:]).then_inc(S.q_h, 1)
+    v.wait_ge(S.ld_w2, 16)
+    v.quantize_mx(T.w2q[:], T.w2s[:], T.w2b[:]).then_inc(S.q_v, 1)
+
+    left = 0
+    if groups:
+        g.wait_ge(S.q_h, 1)
+        for mask, dests in groups:
+            for what in ("s", "q"):
+                left += _write(g, T, topo, r, what, mask, dests, S.sent)
+
+    order = [r] + sorted(arrive, key=lambda j: arrive[j][1])
+    stored = {0: [], 1: []}
+    for i, j in enumerate(order):
+        if j == r:
+            t.wait_ge(S.q_h, 1)
+            t.wait_ge(S.q_v, 1)
+        else:
+            t.wait_ge(S["as%d" % j], arrive[j][0])
+            t.wait_ge(S["aq%d" % j], arrive[j][0])
+        bank = (len(RUNS) + i) % NBANKS
+        p = T.ps[:, BANK * bank:BANK * bank + NC]
+        t.matmul_mx(p, T.w2q[:], T.w2s[:], T.gq[:, _slot(j)], T.gs[:, _slot(j)], True, True).then_inc(S["m%d" % j], 1)
+        if i % 2 == 0:
+            v.wait_ge(S["m%d" % j], 1)
+            v.tensor_copy(T.ysb[:, _slot(j)], p).then_inc(S["c%d" % j], 1)
+            q = sy
+        else:
+            sc.wait_ge(S["m%d" % j], 1)
+            sc.activation(T.ysb[:, _slot(j)], p, ActivationFunctionType.Copy).then_inc(S["c%d" % j], 1)
+            q = sc
+        q.wait_ge(S["c%d" % j], 1)
+        if j == r and left:
+            q.wait_ge(S.sent, left)
+        q.dma_start(T.y[:, _slot(j)], T.ysb[:, _slot(j)]).then_inc(S["st%d" % j], 16)
+        stored[i % 2].append(j)
+    for i, q in ((0, sy), (1, sc)):
+        for j in stored[i]:
+            q.wait_ge(S["st%d" % j], 16)
+    if left:
+        g.wait_ge(S.sent, left)
+
+
+def rank_program(g, core, T, topo):
+    sends, relays, arrive = _plan(T, topo)
+    r = T.rank_of(core)
+    if r is not None:
+        _rank(g, T, topo, r, sends[r], arrive[r])
+    elif core in relays:
+        _relay(g, T, topo, relays[core])

@@ -3,20 +3,20 @@ from concourse.mybir import dt, AluOpType, ActivationFunctionType
 
 N = 6
 NC = 256
+HALVES = 2
+HC = NC // HALVES
 G = 4
 WC = 128
 C = 0.023
 BANK = 512
 NBANKS = 8
-
-OWN_DIE = {(0, 5): False, (0, 3): True, (0, 1): True,
-           (1, 4): False, (1, 2): True,
-           (2, 5): True, (2, 3): False,
-           (3, 4): False,
-           (4, 5): False}
 ENGINES = 8
 
-RUNS = [(0, 0, NC), (1, 0, NC), (2, 0, NC), (3, 0, NC // 2), (3, NC // 2, NC)]
+NEAR = {0: [(False, [5]), (True, [3, 1])],
+        1: [(False, [4]), (True, [2])],
+        2: [(False, [5]), (False, [3])],
+        3: [(False, [4])]}
+FAR = {4: [(True, 5)]}
 
 SCRATCH = {
     "xb": ("sbuf", [128, 4 * NC], "bfloat16"),
@@ -34,11 +34,11 @@ SCRATCH = {
     "ysb": ("sbuf", [128, N * NC], "float32"),
     "ps": ("psum", [128, NBANKS * BANK], "float32"),
 }
-SEMAPHORES = (["ld_x", "ld_wa", "ld_wb", "ld_w2", "q_x", "q_v", "q_h", "sent"]
+_PIECES = ["%d_%d" % (j, a) for j in range(N) for a in range(HALVES)]
+SEMAPHORES = (["ld_x0", "ld_x1", "ld_wa", "ld_wb", "ld_w2", "q_x0", "q_x1", "q_v", "q_h0", "q_h1", "sent"]
               + ["q_w%d" % i for i in range(G)]
-              + ["z%d" % k for k in range(len(RUNS))] + ["a%d" % k for k in range(len(RUNS))]
-              + ["as%d" % j for j in range(N)] + ["aq%d" % j for j in range(N)]
-              + ["m%d" % j for j in range(N)] + ["c%d" % j for j in range(N)] + ["st%d" % j for j in range(N)])
+              + ["z%d" % k for k in range(HALVES * G)] + ["a%d" % k for k in range(HALVES * G)]
+              + [p + k for p in ("as", "aq", "m", "c", "st") for k in _PIECES])
 
 
 def _count(mask):
@@ -58,72 +58,88 @@ def _plan(T, topo):
     every = range(topo.CHIPS * topo.CORES_PER_CHIP)
     sends, relays, arrive = {}, {}, dict((r, {}) for r in range(N))
     for j, src in enumerate(cores):
-        groups, queued = [], [0, 0]
-        direct = [r for r in range(N - 1, j, -1) if topo.may_write(src, cores[r])]
-        for n, r in enumerate(r for r in range(N - 1, j, -1) if r not in direct):
-            dst = cores[r]
+        leave = topo.mask(src, cores[(j + 1) % N])
+        stay_dests, leave_dests, served = [], [], set()
+        stay = 0
+        for own, rs in NEAR.get(j, []):
             relay = [c for c in every
                      if topo.chip(c) == topo.chip(src) and T.rank_of(c) is None and c not in relays
-                     and topo.may_write(c, dst) and (topo.die(c) == topo.die(src)) == OWN_DIE[(j, r)]][0]
-            s = n % 2
-            leave = topo.mask(src, dst)
-            mask = _take(topo.mask(src, relay) & (leave if s else ~leave), ENGINES)
-            out = _take(topo.mask(relay, dst), ENGINES)
-            relays[relay] = (j, dst, _count(mask), out)
-            groups.append((mask, [relay]))
-            queued[s] += 1
-            arrive[r][j] = (_count(out), queued[s] + 4.0 - 0.01 * j)
-        if direct:
-            mask = _take(topo.mask(src, cores[direct[0]]), ENGINES)
-            groups.append((mask, [cores[r] for r in direct]))
-            for r in direct:
-                queued[1] += 1
-                arrive[r][j] = (_count(mask), queued[1] + 1.5 - 0.01 * j)
-        sends[j] = groups
+                     and all(topo.may_write(c, cores[r]) for r in rs)
+                     and (topo.die(c) == topo.die(src)) == own][0]
+            stay = _take(topo.mask(src, relay) & ~leave, ENGINES)
+            out = _take(topo.mask(relay, cores[rs[0]]), ENGINES)
+            relays[relay] = (j, [cores[r] for r in rs], _count(stay), out)
+            for n, r in enumerate(rs):
+                arrive[r][j] = (_count(out), 3.0 + len(stay_dests) + n - 0.01 * j)
+                served.add(r)
+            stay_dests.append(relay)
+        go = _take(leave, ENGINES)
+        for own, r in FAR.get(j, []):
+            relay = [c for c in every
+                     if topo.mates(topo.chip(c), topo.chip(cores[r])) and T.rank_of(c) is None and c not in relays
+                     and topo.may_write(src, c) and topo.may_write(c, cores[r])
+                     and (topo.die(c) == topo.die(src)) == own][0]
+            out = _take(topo.mask(relay, cores[r]), ENGINES)
+            relays[relay] = (j, [cores[r]], _count(go), out)
+            arrive[r][j] = (_count(out), 2.5 + len(leave_dests) - 0.01 * j)
+            served.add(r)
+            leave_dests.append(relay)
+        for r in range(N - 1, j, -1):
+            if r not in served:
+                arrive[r][j] = (_count(go), 0.0 + len(leave_dests) - 0.01 * j)
+                leave_dests.append(cores[r])
+        sends[j] = [(m, d) for m, d in ((stay, stay_dests), (go, leave_dests)) if d]
     return sends, relays, arrive
 
 
-def _slot(j):
-    return slice(NC * j, NC * j + NC)
+def _cols(j, a):
+    return slice(NC * j + HC * a, NC * j + HC * a + HC)
 
 
-def _write(g, T, topo, j, what, mask, dests, local_sem):
+def _write(g, T, topo, j, a, what, transfers, local_sem):
+    key = "%d_%d" % (j, a)
     if what == "s":
-        view, sem = T.gs[:, _slot(j)], T.sem["as%d" % j]
+        view, sem = T.gs[:, _cols(j, a)], T.sem["as" + key]
     else:
-        view, sem = T.gq[:, _slot(j)].bitcast(dt.uint8), T.sem["aq%d" % j]
-    if len(dests) == 1:
+        view, sem = T.gq[:, _cols(j, a)].bitcast(dt.uint8), T.sem["aq" + key]
+    if len(transfers) == 1 and len(transfers[0][1]) == 1:
+        mask, dests = transfers[0]
         rid, pid, _ = topo.addr(dests[0])
         g.remote_dma(out_ap=view, in_ap=view, remote_sem=sem, local_sem=local_sem, pid=pid, routing_id=rid,
                      dma_engine_mask=mask)
     else:
-        ids = [DstId(rid=topo.addr(d)[0], pnc=topo.addr(d)[1]) for d in dests]
-        g.remote_dma_fused([RemoteDMATransfer(dst_ids=ids, dma_engine_mask=mask, remote_sem=sem, srcs=[view],
-                                              dsts=[view for _ in dests])], local_sem=local_sem)
-    return _count(mask)
+        g.remote_dma_fused([RemoteDMATransfer(dst_ids=[DstId(rid=topo.addr(d)[0], pnc=topo.addr(d)[1]) for d in dests],
+                                              dma_engine_mask=mask, remote_sem=sem, srcs=[view],
+                                              dsts=[view for _ in dests])
+                            for mask, dests in transfers], local_sem=local_sem)
+    return sum(_count(mask) for mask, _ in transfers)
 
 
 def _relay(g, T, topo, job):
-    j, dst, n_in, out = job
+    j, dests, n_in, out = job
     left = 0
-    for what in ("s", "q"):
-        g.wait_ge(T.sem["a%s%d" % (what, j)], n_in)
-        left += _write(g, T, topo, j, what, out, [dst], T.sem.sent)
+    for a in range(HALVES):
+        for what in ("s", "q"):
+            g.wait_ge(T.sem["a%s%d_%d" % (what, j, a)], n_in)
+            left += _write(g, T, topo, j, a, what, [(out, dests)], T.sem.sent)
     g.wait_ge(T.sem.sent, left)
 
 
-def _rank(g, T, topo, r, groups, arrive):
+def _rank(g, T, topo, r, transfers, arrive):
     S = T.sem
     v, t, sc, sy = g.vector, g.tensor, g.scalar, g.sync
-    half = G * 4 * WC // 2
+    wh = G * 4 * WC // 2
+    xh = 4 * HC
 
-    sy.dma_start(T.xb[:], T.x[:]).then_inc(S.ld_x, 16)
-    sc.dma_start(T.w1b[:, 0:half], T.w1[:, 0:half]).then_inc(S.ld_wa, 16)
-    sy.dma_start(T.w1b[:, half:2 * half], T.w1[:, half:2 * half]).then_inc(S.ld_wb, 16)
+    sy.dma_start(T.xb[:, 0:xh], T.x[:, 0:xh]).then_inc(S.ld_x0, 16)
+    sc.dma_start(T.w1b[:, 0:wh], T.w1[:, 0:wh]).then_inc(S.ld_wa, 16)
+    sy.dma_start(T.w1b[:, wh:2 * wh], T.w1[:, wh:2 * wh]).then_inc(S.ld_wb, 16)
+    sy.dma_start(T.xb[:, xh:2 * xh], T.x[:, xh:2 * xh]).then_inc(S.ld_x1, 16)
+    sc.wait_ge(S.ld_wa, 16)
     sc.dma_start(T.w2b[:], T.w2[:]).then_inc(S.ld_w2, 16)
 
-    v.wait_ge(S.ld_x, 16)
-    v.quantize_mx(T.xq[:], T.xs[:], T.xb[:]).then_inc(S.q_x, 1)
+    v.wait_ge(S.ld_x0, 16)
+    v.quantize_mx(T.xq[:, 0:HC], T.xs[:, 0:HC], T.xb[:, 0:xh]).then_inc(S.q_x0, 1)
     for i in range(G):
         if i == 0:
             v.wait_ge(S.ld_wa, 16)
@@ -131,62 +147,73 @@ def _rank(g, T, topo, r, groups, arrive):
             v.wait_ge(S.ld_wb, 16)
         v.quantize_mx(T.w1q[:, WC * i:WC * i + WC], T.w1s[:, WC * i:WC * i + WC],
                       T.w1b[:, 4 * WC * i:4 * WC * i + 4 * WC]).then_inc(S["q_w%d" % i], 1)
+    v.wait_ge(S.ld_x1, 16)
+    v.quantize_mx(T.xq[:, HC:2 * HC], T.xs[:, HC:2 * HC], T.xb[:, xh:2 * xh]).then_inc(S.q_x1, 1)
 
-    t.wait_ge(S.q_x, 1)
-    for k, (b, c0, c1) in enumerate(RUNS):
-        if c0 == 0:
-            t.wait_ge(S["q_w%d" % b], 1)
-        z = T.ps[:, BANK * k:BANK * k + (c1 - c0)]
-        t.matmul_mx(z, T.w1q[:, WC * b:WC * b + WC], T.w1s[:, WC * b:WC * b + WC],
-                    T.xq[:, c0:c1], T.xs[:, c0:c1], True, True).then_inc(S["z%d" % k], 1)
-        h = T.hb[:, 4 * c0 + b:4 * c1:4]
-        if k < len(RUNS) - 1:
-            sc.wait_ge(S["z%d" % k], 1)
-            sc.activation(h, z, ActivationFunctionType.Relu, scale=C).then_inc(S["a%d" % k], 1)
-        else:
-            v.wait_ge(S["z%d" % k], 1)
-            v.tensor_scalar(h, z, 0.0, C, AluOpType.max, AluOpType.mult).then_inc(S["a%d" % k], 1)
-    for k in range(len(RUNS)):
-        v.wait_ge(S["a%d" % k], 1)
-    v.quantize_mx(T.gq[:, _slot(r)], T.gs[:, _slot(r)], T.hb[:]).then_inc(S.q_h, 1)
+    for a in range(HALVES):
+        t.wait_ge(S["q_x%d" % a], 1)
+        for b in range(G):
+            if a == 0:
+                t.wait_ge(S["q_w%d" % b], 1)
+            k = G * a + b
+            z = T.ps[:, BANK * k:BANK * k + HC]
+            t.matmul_mx(z, T.w1q[:, WC * b:WC * b + WC], T.w1s[:, WC * b:WC * b + WC],
+                        T.xq[:, HC * a:HC * a + HC], T.xs[:, HC * a:HC * a + HC], True, True).then_inc(S["z%d" % k], 1)
+            h = T.hb[:, xh * a + b:xh * a + xh:4]
+            if a == 1 and b % 2 == 1:
+                v.wait_ge(S["z%d" % k], 1)
+                v.tensor_scalar(h, z, 0.0, C, AluOpType.max, AluOpType.mult).then_inc(S["a%d" % k], 1)
+            else:
+                sc.wait_ge(S["z%d" % k], 1)
+                sc.activation(h, z, ActivationFunctionType.Relu, scale=C).then_inc(S["a%d" % k], 1)
+        for b in range(G):
+            v.wait_ge(S["a%d" % (G * a + b)], 1)
+        v.quantize_mx(T.gq[:, _cols(r, a)], T.gs[:, _cols(r, a)],
+                      T.hb[:, xh * a:xh * a + xh]).then_inc(S["q_h%d" % a], 1)
     v.wait_ge(S.ld_w2, 16)
     v.quantize_mx(T.w2q[:], T.w2s[:], T.w2b[:]).then_inc(S.q_v, 1)
 
     left = 0
-    if groups:
-        g.wait_ge(S.q_h, 1)
-        for mask, dests in groups:
+    if transfers:
+        for a in range(HALVES):
+            g.wait_ge(S["q_h%d" % a], 1)
             for what in ("s", "q"):
-                left += _write(g, T, topo, r, what, mask, dests, S.sent)
+                left += _write(g, T, topo, r, a, what, transfers, S.sent)
 
-    order = [r] + sorted(arrive, key=lambda j: arrive[j][1])
+    others = sorted(arrive, key=lambda j: arrive[j][1])
+    jobs = [(r, 0, NC)] + [(j, a, HC) for a in range(HALVES) for j in others]
     stored = {0: [], 1: []}
-    for i, j in enumerate(order):
+    for i, (j, a, n) in enumerate(jobs):
+        key = "%d_%d" % (j, a)
         if j == r:
-            t.wait_ge(S.q_h, 1)
+            for h in range(HALVES):
+                t.wait_ge(S["q_h%d" % h], 1)
             t.wait_ge(S.q_v, 1)
         else:
-            t.wait_ge(S["as%d" % j], arrive[j][0])
-            t.wait_ge(S["aq%d" % j], arrive[j][0])
-        bank = (len(RUNS) + i) % NBANKS
-        p = T.ps[:, BANK * bank:BANK * bank + NC]
-        t.matmul_mx(p, T.w2q[:], T.w2s[:], T.gq[:, _slot(j)], T.gs[:, _slot(j)], True, True).then_inc(S["m%d" % j], 1)
+            t.wait_ge(S["as" + key], arrive[j][0])
+            t.wait_ge(S["aq" + key], arrive[j][0])
+        if i >= NBANKS:
+            t.wait_ge(S["c%d_%d" % jobs[i - NBANKS][:2]], 1)
+        c0 = NC * j + HC * a
+        bank = i % NBANKS
+        p = T.ps[:, BANK * bank:BANK * bank + n]
+        t.matmul_mx(p, T.w2q[:], T.w2s[:], T.gq[:, c0:c0 + n], T.gs[:, c0:c0 + n], True, True).then_inc(S["m" + key], 1)
         if i % 2 == 0:
-            v.wait_ge(S["m%d" % j], 1)
-            v.tensor_copy(T.ysb[:, _slot(j)], p).then_inc(S["c%d" % j], 1)
+            v.wait_ge(S["m" + key], 1)
+            v.tensor_copy(T.ysb[:, c0:c0 + n], p).then_inc(S["c" + key], 1)
             q = sy
         else:
-            sc.wait_ge(S["m%d" % j], 1)
-            sc.activation(T.ysb[:, _slot(j)], p, ActivationFunctionType.Copy).then_inc(S["c%d" % j], 1)
+            sc.wait_ge(S["m" + key], 1)
+            sc.activation(T.ysb[:, c0:c0 + n], p, ActivationFunctionType.Copy).then_inc(S["c" + key], 1)
             q = sc
-        q.wait_ge(S["c%d" % j], 1)
+        q.wait_ge(S["c" + key], 1)
         if j == r and left:
             q.wait_ge(S.sent, left)
-        q.dma_start(T.y[:, _slot(j)], T.ysb[:, _slot(j)]).then_inc(S["st%d" % j], 16)
-        stored[i % 2].append(j)
+        q.dma_start(T.y[:, c0:c0 + n], T.ysb[:, c0:c0 + n]).then_inc(S["st" + key], 16)
+        stored[i % 2].append(key)
     for i, q in ((0, sy), (1, sc)):
-        for j in stored[i]:
-            q.wait_ge(S["st%d" % j], 16)
+        for key in stored[i]:
+            q.wait_ge(S["st" + key], 16)
     if left:
         g.wait_ge(S.sent, left)
 

from concourse.bass import DstId, RemoteDMATransfer
from concourse.mybir import dt, AluOpType, ActivationFunctionType

N = 6
NC = 256
HALVES = 2
HC = NC // HALVES
G = 4
WC = 128
C = 0.023
BANK = 512
NBANKS = 8
ENGINES = 8

NEAR = {0: [(False, [5]), (True, [3, 1])],
        1: [(False, [4]), (True, [2])],
        2: [(False, [5]), (False, [3])],
        3: [(False, [4])]}
FAR = {4: [(True, 5)]}

SCRATCH = {
    "xb": ("sbuf", [128, 4 * NC], "bfloat16"),
    "w1b": ("sbuf", [128, G * 4 * WC], "bfloat16"),
    "w2b": ("sbuf", [128, 4 * WC], "bfloat16"),
    "hb": ("sbuf", [128, 4 * NC], "bfloat16"),
    "xq": ("sbuf", [128, NC], "float8_e4m3fn_x4"),
    "xs": ("sbuf", [128, NC], "uint8"),
    "w1q": ("sbuf", [128, G * WC], "float8_e4m3fn_x4"),
    "w1s": ("sbuf", [128, G * WC], "uint8"),
    "w2q": ("sbuf", [128, WC], "float8_e4m3fn_x4"),
    "w2s": ("sbuf", [128, WC], "uint8"),
    "gq": ("sbuf", [128, N * NC], "float8_e4m3fn_x4"),
    "gs": ("sbuf", [128, N * NC], "uint8"),
    "ysb": ("sbuf", [128, N * NC], "float32"),
    "ps": ("psum", [128, NBANKS * BANK], "float32"),
}
_PIECES = ["%d_%d" % (j, a) for j in range(N) for a in range(HALVES)]
SEMAPHORES = (["ld_x0", "ld_x1", "ld_wa", "ld_wb", "ld_w2", "q_x0", "q_x1", "q_v", "q_h0", "q_h1", "sent"]
              + ["q_w%d" % i for i in range(G)]
              + ["z%d" % k for k in range(HALVES * G)] + ["a%d" % k for k in range(HALVES * G)]
              + [p + k for p in ("as", "aq", "m", "c", "st") for k in _PIECES])


def _count(mask):
    return bin(mask).count("1")


def _take(mask, k):
    out = 0
    for e in range(mask.bit_length()):
        if (mask >> e) & 1 and _count(out) < k:
            out |= 1 << e
    return out


def _plan(T, topo):
    cores = list(T.cores)
    every = range(topo.CHIPS * topo.CORES_PER_CHIP)
    sends, relays, arrive = {}, {}, dict((r, {}) for r in range(N))
    for j, src in enumerate(cores):
        leave = topo.mask(src, cores[(j + 1) % N])
        stay_dests, leave_dests, served = [], [], set()
        stay = 0
        for own, rs in NEAR.get(j, []):
            relay = [c for c in every
                     if topo.chip(c) == topo.chip(src) and T.rank_of(c) is None and c not in relays
                     and all(topo.may_write(c, cores[r]) for r in rs)
                     and (topo.die(c) == topo.die(src)) == own][0]
            stay = _take(topo.mask(src, relay) & ~leave, ENGINES)
            out = _take(topo.mask(relay, cores[rs[0]]), ENGINES)
            relays[relay] = (j, [cores[r] for r in rs], _count(stay), out)
            for n, r in enumerate(rs):
                arrive[r][j] = (_count(out), 3.0 + len(stay_dests) + n - 0.01 * j)
                served.add(r)
            stay_dests.append(relay)
        go = _take(leave, ENGINES)
        for own, r in FAR.get(j, []):
            relay = [c for c in every
                     if topo.mates(topo.chip(c), topo.chip(cores[r])) and T.rank_of(c) is None and c not in relays
                     and topo.may_write(src, c) and topo.may_write(c, cores[r])
                     and (topo.die(c) == topo.die(src)) == own][0]
            out = _take(topo.mask(relay, cores[r]), ENGINES)
            relays[relay] = (j, [cores[r]], _count(go), out)
            arrive[r][j] = (_count(out), 2.5 + len(leave_dests) - 0.01 * j)
            served.add(r)
            leave_dests.append(relay)
        for r in range(N - 1, j, -1):
            if r not in served:
                arrive[r][j] = (_count(go), 0.0 + len(leave_dests) - 0.01 * j)
                leave_dests.append(cores[r])
        sends[j] = [(m, d) for m, d in ((stay, stay_dests), (go, leave_dests)) if d]
    return sends, relays, arrive


def _cols(j, a):
    return slice(NC * j + HC * a, NC * j + HC * a + HC)


def _write(g, T, topo, j, a, what, transfers, local_sem):
    key = "%d_%d" % (j, a)
    if what == "s":
        view, sem = T.gs[:, _cols(j, a)], T.sem["as" + key]
    else:
        view, sem = T.gq[:, _cols(j, a)].bitcast(dt.uint8), T.sem["aq" + key]
    if len(transfers) == 1 and len(transfers[0][1]) == 1:
        mask, dests = transfers[0]
        rid, pid, _ = topo.addr(dests[0])
        g.remote_dma(out_ap=view, in_ap=view, remote_sem=sem, local_sem=local_sem, pid=pid, routing_id=rid,
                     dma_engine_mask=mask)
    else:
        g.remote_dma_fused([RemoteDMATransfer(dst_ids=[DstId(rid=topo.addr(d)[0], pnc=topo.addr(d)[1]) for d in dests],
                                              dma_engine_mask=mask, remote_sem=sem, srcs=[view],
                                              dsts=[view for _ in dests])
                            for mask, dests in transfers], local_sem=local_sem)
    return sum(_count(mask) for mask, _ in transfers)


def _relay(g, T, topo, job):
    j, dests, n_in, out = job
    left = 0
    for a in range(HALVES):
        for what in ("s", "q"):
            g.wait_ge(T.sem["a%s%d_%d" % (what, j, a)], n_in)
            left += _write(g, T, topo, j, a, what, [(out, dests)], T.sem.sent)
    g.wait_ge(T.sem.sent, left)


def _rank(g, T, topo, r, transfers, arrive):
    S = T.sem
    v, t, sc, sy = g.vector, g.tensor, g.scalar, g.sync
    wh = G * 4 * WC // 2
    xh = 4 * HC

    sy.dma_start(T.xb[:, 0:xh], T.x[:, 0:xh]).then_inc(S.ld_x0, 16)
    sc.dma_start(T.w1b[:, 0:wh], T.w1[:, 0:wh]).then_inc(S.ld_wa, 16)
    sy.dma_start(T.w1b[:, wh:2 * wh], T.w1[:, wh:2 * wh]).then_inc(S.ld_wb, 16)
    sy.dma_start(T.xb[:, xh:2 * xh], T.x[:, xh:2 * xh]).then_inc(S.ld_x1, 16)
    sc.wait_ge(S.ld_wa, 16)
    sc.dma_start(T.w2b[:], T.w2[:]).then_inc(S.ld_w2, 16)

    v.wait_ge(S.ld_x0, 16)
    v.quantize_mx(T.xq[:, 0:HC], T.xs[:, 0:HC], T.xb[:, 0:xh]).then_inc(S.q_x0, 1)
    for i in range(G):
        if i == 0:
            v.wait_ge(S.ld_wa, 16)
        if i == G // 2:
            v.wait_ge(S.ld_wb, 16)
        v.quantize_mx(T.w1q[:, WC * i:WC * i + WC], T.w1s[:, WC * i:WC * i + WC],
                      T.w1b[:, 4 * WC * i:4 * WC * i + 4 * WC]).then_inc(S["q_w%d" % i], 1)
    v.wait_ge(S.ld_x1, 16)
    v.quantize_mx(T.xq[:, HC:2 * HC], T.xs[:, HC:2 * HC], T.xb[:, xh:2 * xh]).then_inc(S.q_x1, 1)

    for a in range(HALVES):
        t.wait_ge(S["q_x%d" % a], 1)
        for b in range(G):
            if a == 0:
                t.wait_ge(S["q_w%d" % b], 1)
            k = G * a + b
            z = T.ps[:, BANK * k:BANK * k + HC]
            t.matmul_mx(z, T.w1q[:, WC * b:WC * b + WC], T.w1s[:, WC * b:WC * b + WC],
                        T.xq[:, HC * a:HC * a + HC], T.xs[:, HC * a:HC * a + HC], True, True).then_inc(S["z%d" % k], 1)
            h = T.hb[:, xh * a + b:xh * a + xh:4]
            if a == 1 and b % 2 == 1:
                v.wait_ge(S["z%d" % k], 1)
                v.tensor_scalar(h, z, 0.0, C, AluOpType.max, AluOpType.mult).then_inc(S["a%d" % k], 1)
            else:
                sc.wait_ge(S["z%d" % k], 1)
                sc.activation(h, z, ActivationFunctionType.Relu, scale=C).then_inc(S["a%d" % k], 1)
        for b in range(G):
            v.wait_ge(S["a%d" % (G * a + b)], 1)
        v.quantize_mx(T.gq[:, _cols(r, a)], T.gs[:, _cols(r, a)],
                      T.hb[:, xh * a:xh * a + xh]).then_inc(S["q_h%d" % a], 1)
    v.wait_ge(S.ld_w2, 16)
    v.quantize_mx(T.w2q[:], T.w2s[:], T.w2b[:]).then_inc(S.q_v, 1)

    left = 0
    if transfers:
        for a in range(HALVES):
            g.wait_ge(S["q_h%d" % a], 1)
            for what in ("s", "q"):
                left += _write(g, T, topo, r, a, what, transfers, S.sent)

    others = sorted(arrive, key=lambda j: arrive[j][1])
    jobs = [(r, 0, NC)] + [(j, a, HC) for a in range(HALVES) for j in others]
    stored = {0: [], 1: []}
    for i, (j, a, n) in enumerate(jobs):
        key = "%d_%d" % (j, a)
        if j == r:
            for h in range(HALVES):
                t.wait_ge(S["q_h%d" % h], 1)
            t.wait_ge(S.q_v, 1)
        else:
            t.wait_ge(S["as" + key], arrive[j][0])
            t.wait_ge(S["aq" + key], arrive[j][0])
        if i >= NBANKS:
            t.wait_ge(S["c%d_%d" % jobs[i - NBANKS][:2]], 1)
        c0 = NC * j + HC * a
        bank = i % NBANKS
        p = T.ps[:, BANK * bank:BANK * bank + n]
        t.matmul_mx(p, T.w2q[:], T.w2s[:], T.gq[:, c0:c0 + n], T.gs[:, c0:c0 + n], True, True).then_inc(S["m" + key], 1)
        if i % 2 == 0:
            v.wait_ge(S["m" + key], 1)
            v.tensor_copy(T.ysb[:, c0:c0 + n], p).then_inc(S["c" + key], 1)
            q = sy
        else:
            sc.wait_ge(S["m" + key], 1)
            sc.activation(T.ysb[:, c0:c0 + n], p, ActivationFunctionType.Copy).then_inc(S["c" + key], 1)
            q = sc
        q.wait_ge(S["c" + key], 1)
        if j == r and left:
            q.wait_ge(S.sent, left)
        q.dma_start(T.y[:, c0:c0 + n], T.ysb[:, c0:c0 + n]).then_inc(S["st" + key], 16)
        stored[i % 2].append(key)
    for i, q in ((0, sy), (1, sc)):
        for key in stored[i]:
            q.wait_ge(S["st" + key], 16)
    if left:
        g.wait_ge(S.sent, left)


def rank_program(g, core, T, topo):
    sends, relays, arrive = _plan(T, topo)
    r = T.rank_of(core)
    if r is not None:
        _rank(g, T, topo, r, sends[r], arrive[r])
    elif core in relays:
        _relay(g, T, topo, relays[core])
